import numpy as np
import ml_dtypes


def mxq(x, axis, fmt="e4m3"):
    dtype, down = {"e4m3": (ml_dtypes.float8_e4m3fn, 7), "e5m2": (ml_dtypes.float8_e5m2, 14)}[fmt]
    v = np.moveaxis(np.asarray(x, np.float32).astype(ml_dtypes.bfloat16).astype(np.float64), axis, -1)
    blocks = v.reshape(v.shape[:-1] + (-1, 32))
    amax = np.abs(blocks).max(-1, keepdims=True)
    byte = np.maximum(np.where(amax > 0, np.frexp(amax)[1] - 1 + 127, 0) - down, 1)
    scale = np.exp2(byte - 127.0)
    codes = (blocks / scale).astype(np.float32).astype(dtype).astype(np.float64)
    return np.moveaxis((codes * scale).reshape(v.shape), -1, axis)


WIDE = False


def mx_kscale(k):
    if not WIDE:
        return np.ones(k)
    levels = np.array([10, -10, 5, -5, 0])
    if k % 512:
        return np.exp2(np.random.permutation(np.resize(levels, k // 32))).repeat(32)
    a = np.empty((k // 512, 16))
    for p in range(k // 512):
        a[p, :8] = np.random.permutation(np.resize(levels, 8))
        for g in range(8):
            far = levels[np.abs(levels - a[p, g]) >= 10]
            a[p, g + 8] = far[np.random.randint(len(far))]
    return np.exp2(a.ravel()).repeat(32)


def f64(x):
    return np.asarray(x).astype(np.float64)


def striped(idx):
    return np.tile(idx.reshape(-1, 16).T, (8, 1)).astype(np.uint16)


def unstriped(offs):
    return offs[:16].T.reshape(-1).astype(np.int64)


def pack_weight(w):
    k, n = w.shape
    w = f64(np.asarray(w, np.float32).astype(ml_dtypes.bfloat16)).reshape(k // 32, 32, n)
    amax = np.abs(w).max(1)
    byte = np.clip(np.where(amax > 0, np.frexp(amax)[1] - 1 + 127 - 7, 1), 1, 254)
    scaled = (w * np.exp2(127.0 - byte)[:, None, :]).reshape(k, n).astype(np.float32)
    words = np.ascontiguousarray(scaled.reshape(k // 512, 128, 4, n).transpose(0, 1, 3, 2)).astype(ml_dtypes.float8_e4m3fn).view(np.uint8)
    return words, np.ascontiguousarray(byte.astype(np.uint8).reshape(k // 512, 16, n))


def unpack_weight(words, scales):
    g, p, n, _ = words.shape
    vals = np.ascontiguousarray(words).view(ml_dtypes.float8_e4m3fn).astype(np.float64) * np.repeat(np.exp2(scales.astype(np.float64) - 127.0), 8, axis=1)[..., None]
    return vals.transpose(0, 1, 3, 2).reshape(g * 512, n)


def relu(v):
    return np.maximum(v, 0.0)


K, T, S, V, R, W = 512, 2048, 512, 512, 256, 1024
P = 2 ** 7


def setup_inputs():
    n = np.random.standard_normal
    s = mx_kscale(K)[:, None]
    packed_xT = pack_weight(n((K, T)) * s)
    packed_eT = pack_weight(n((K, W)) * s)
    return {
        "x_words": packed_xT[0],
        "x_scales": packed_xT[1],
        "hT": (n((K, V)) / np.sqrt(K) / s).astype(np.float32),
        "e_words": packed_eT[0],
        "e_scales": packed_eT[1],
        "totl": (np.tile(np.random.uniform(150.0, 300.0, W), (P, 1))).astype(np.float32),
        "bow": (np.tile(np.random.uniform(0.2, 0.7, T), (P, 1))).astype(np.float32),
        "tot": (np.tile(np.random.uniform(20.0, 60.0, T), (P, 1))).astype(np.float32),
        "offs": striped(np.random.permutation(T)[:S]),
        "low": striped(np.random.permutation(W)[:R]),
        "suf": striped(np.random.permutation(np.concatenate([np.arange(R), np.random.randint(0, R, S - R)]))),
    }


def reference(x_words, x_scales, hT, e_words, e_scales, totl, bow, tot, offs, low, suf):
    hTq = mxq(f64(hT), 0, "e4m3")
    xq = unpack_weight(x_words, x_scales)[:, unstriped(offs)]
    y = hTq.T @ xq
    ca = np.exp(0.8 * y)
    da = relu(ca - 0.75)
    e_low = unpack_weight(e_words, e_scales)[:, unstriped(low)]
    z = hTq.T @ e_low
    cl = np.exp(0.8 * z)
    tl = f64(totl)[:1][:, unstriped(low)]
    plow = cl / tl
    return np.log(100.0 * (da / (f64(tot)[:1][:, unstriped(offs)]) + (f64(bow)[:1][:, unstriped(offs)]) * plow[:, unstriped(suf)]) + 0.05)

@@ -1,0 +1,202 @@
+from contextlib import ExitStack
+
+import concourse.mybir as mybir
+from concourse.masks import make_identity
+
+K, T, S, V, R, W = 512, 2048, 512, 512, 256, 1024
+FLOPS = 2 * K * V * (S + R)
+
+F32 = mybir.dt.float32
+BF16 = mybir.dt.bfloat16
+I32 = mybir.dt.int32
+U32 = mybir.dt.uint32
+U16 = mybir.dt.uint16
+U8 = mybir.dt.uint8
+FP8X4 = mybir.dt.float8_e4m3fn_x4
+ACT = mybir.ActivationFunctionType
+ALU = mybir.AluOpType
+
+P = 128
+PACK = 4
+HALF = V // 2
+WINDOW = S + 16
+TOT_ROW, BOW_ROW, TOTL_ROW = 0, 4, 8
+
+
+def tile_picked_ybackof_log_p_kernel(
+    tc, x_words, x_scales, hT, e_words, e_scales, totl, bow, tot, offs, low, suf, out
+):
+    nc = tc.nc
+    with ExitStack() as ctx:
+        keep = ctx.enter_context(tc.tile_pool(name="keep", bufs=1))
+        ubanks = ctx.enter_context(tc.psum_pool(name="ubanks", bufs=4))
+        wbanks = ctx.enter_context(tc.psum_pool(name="wbanks", bufs=4))
+
+        low_sb = keep.tile([P, R // 16], U16, name="low_sb")
+        offs_sb = keep.tile([P, S // 16], U16, name="offs_sb")
+        suf_sb = keep.tile([P, S // 16], U16, name="suf_sb")
+        rows = keep.tile([P, T], F32, name="rows")
+        e_bytes = keep.tile([P, W], U8, name="e_bytes")
+        x_bytes = keep.tile([P, T], U8, name="x_bytes")
+        e_table = keep.tile([P, W], I32, name="e_table")
+        x_table = keep.tile([P, T], I32, name="x_table")
+        h_raw = [keep.tile([P, PACK, HALF], F32, name=f"h_raw{h}") for h in range(2)]
+        windows = [keep.tile([P, WINDOW], F32, name=f"window{b}") for b in range(4)]
+        ident = keep.tile([P, P], F32, name="ident")
+        warm = keep.tile([P, 1], F32, name="warm")
+        warm2 = keep.tile([P, 1], F32, name="warm2")
+
+        nc.vector.memset(warm[:], 0.0)
+        nc.vector.memset(e_bytes[:].bitcast(I32), 0)
+        nc.vector.memset(x_bytes[:].bitcast(I32), 0)
+        nc.vector.memset(rows[:].bitcast(I32), 0)
+        for b in range(4):
+            nc.vector.memset(windows[b][:, 2 * R : WINDOW], 0.0)
+        nc.scalar.activation(warm2[:], warm[:], ACT.Exp)
+        make_identity(nc, ident[:])
+
+        h_view = hT.rearrange("(p j) w -> p j w", j=PACK)
+        nc.sync.dma_start(low_sb[:], low)
+        nc.sync.dma_start(e_table[:], e_words[0].rearrange("p n t -> p (n t)").bitcast(I32))
+        for q in range(4):
+            nc.sync.dma_start(
+                e_bytes[32 * q : 32 * q + 4, :].bitcast(I32), e_scales[0, 4 * q : 4 * q + 4, :].bitcast(I32)
+            )
+        nc.sync.dma_start(offs_sb[:], offs)
+        nc.sync.dma_start(h_raw[0][:], h_view[:, :, 0:HALF])
+        nc.scalar.dma_start(rows[TOTL_ROW : TOTL_ROW + 1, 0:W], totl[0:1, :])
+        nc.scalar.dma_start(rows[TOT_ROW : TOT_ROW + 1, :], tot[0:1, :])
+        nc.scalar.dma_start(rows[BOW_ROW : BOW_ROW + 1, :], bow[0:1, :])
+        nc.sync.dma_start(h_raw[1][:], h_view[:, :, HALF:V])
+        nc.sync.dma_start(x_table[:], x_words[0].rearrange("p n t -> p (n t)").bitcast(I32))
+        nc.sync.dma_start(suf_sb[:], suf)
+        for q in range(4):
+            nc.gpsimd.dma_start(
+                x_bytes[32 * q : 32 * q + 4, :].bitcast(I32), x_scales[0, 4 * q : 4 * q + 4, :].bitcast(I32)
+            )
+
+        e_codes = keep.tile([P, R], U32, name="e_codes", align_bytes=64)
+        e_scale = keep.tile([P, R], U8, name="e_scale", align_bytes=64)
+        nc.vector.tensor_copy(e_codes[:], e_table[:].bitcast(U32).indirect(low_sb[:]))
+        nc.vector.tensor_copy(e_scale[:], e_bytes[:].indirect(low_sb[:]))
+
+        by_low = keep.tile([P, R], F32, name="by_low")
+        by_offs = keep.tile([P, S], F32, name="by_offs")
+        nc.vector.tensor_copy(by_low[:], rows[:].indirect(low_sb[:]))
+        nc.vector.tensor_copy(by_offs[:], rows[:].indirect(offs_sb[:]))
+        low_cols = wbanks.tile([P, 2, P], F32, name="low_cols", tag="w")
+        for g in range(2):
+            nc.tensor.transpose(low_cols[:, g, :], by_low[:, g * P : (g + 1) * P], ident[:])
+        offs_cols = wbanks.tile([P, 4, P], F32, name="offs_cols", tag="w")
+        for c in range(4):
+            nc.tensor.transpose(offs_cols[:, c, :], by_offs[:, c * P : (c + 1) * P], ident[:])
+
+        inv_tl = keep.tile([P, 2], F32, name="inv_tl")
+        inv_tot = keep.tile([P, 4], F32, name="inv_tot")
+        floor = keep.tile([P, 4], F32, name="floor")
+        bow_col = keep.tile([P, 4], F32, name="bow_col")
+        nc.vector.reciprocal(inv_tl[:], low_cols[:, :, TOTL_ROW])
+        nc.vector.reciprocal(inv_tot[:], offs_cols[:, :, TOT_ROW])
+        nc.scalar.copy(bow_col[:], offs_cols[:, :, BOW_ROW])
+        nc.scalar.activation(floor[:], inv_tot[:], ACT.Copy, scale=-0.75)
+
+        h_codes = keep.tile([P, V], U32, name="h_codes", align_bytes=64)
+        h_scale = keep.tile([P, V], U8, name="h_scale", align_bytes=64)
+        for h in range(2):
+            grouped = keep.tile([P, HALF, PACK], BF16, name=f"grouped{h}", align_bytes=64)
+            nc.scalar.copy(
+                grouped[:].rearrange("p (c i) t -> p c t i", i=4),
+                h_raw[h][:].rearrange("p t (c i) -> p c t i", i=4),
+            )
+            cols = slice(h * HALF, (h + 1) * HALF)
+            nc.vector.quantize_mx(
+                out=h_codes[:, cols].bitcast(FP8X4),
+                scales=h_scale[:, cols],
+                in_=grouped[:].rearrange("p w j -> p (w j)"),
+            )
+
+        bow_bank = wbanks.tile([P, S], F32, name="bow_bank", tag="w")
+        for c in range(4):
+            nc.tensor.transpose(bow_bank[:, c * P : (c + 1) * P], bow_col[:, c : c + 1].to_broadcast([P, P]), ident[:])
+        bow_all = keep.tile([P, S], F32, name="bow_all")
+        nc.scalar.copy(bow_all[:], bow_bank[:])
+
+        for h in range(2):
+            cols = slice(h * HALF, (h + 1) * HALF)
+            z_bank = wbanks.tile([P, 2, HALF], F32, name="z_bank", tag="w")
+            for g in range(2):
+                nc.tensor.matmul_mx(
+                    out=z_bank[:, g, :],
+                    lhsT=e_codes[:, g * P : (g + 1) * P].bitcast(FP8X4),
+                    lhsT_scale=e_scale[:, g * P : (g + 1) * P],
+                    rhs=h_codes[:, cols].bitcast(FP8X4),
+                    rhs_scale=h_scale[:, cols],
+                    start=True,
+                    stop=True,
+                )
+            cl = keep.tile([P, 2, HALF], F32, name=f"cl{h}")
+            nc.scalar.activation(cl[:], z_bank[:], ACT.Exp, scale=0.8)
+            plow_t = [windows[2 * h + g][:, R : 2 * R] for g in range(2)]
+            for g in range(2):
+                nc.scalar.activation(plow_t[g], cl[:, g, :], ACT.Copy, scale=inv_tl[:, g : g + 1])
+            plow_bank = wbanks.tile([P, 2, R], F32, name="plow_bank", tag="w")
+            for i in range(2):
+                for g in range(2):
+                    nc.tensor.transpose(
+                        plow_bank[:, i, g * P : (g + 1) * P], plow_t[g][:, i * P : (i + 1) * P], ident[:]
+                    )
+            for i in range(2):
+                nc.scalar.copy(windows[2 * h + i][:, 0:R], plow_bank[:, i, :])
+
+        sums = [ubanks.tile([P, S], F32, name="sums", tag="u") for b in range(4)]
+        x_codes = keep.tile([P, S], U32, name="x_codes", align_bytes=64)
+        x_scale = keep.tile([P, S], U8, name="x_scale", align_bytes=64)
+        nc.vector.tensor_copy(x_scale[:], x_bytes[:].indirect(offs_sb[:]))
+        nc.vector.tensor_copy(x_codes[:], x_table[:].bitcast(U32).indirect(offs_sb[:]))
+
+        scaled = []
+        for c in range(4):
+            y_bank = wbanks.tile([P, V], F32, name="y_bank", tag="w")
+            nc.tensor.matmul_mx(
+                out=y_bank[:],
+                lhsT=x_codes[:, c * P : (c + 1) * P].bitcast(FP8X4),
+                lhsT_scale=x_scale[:, c * P : (c + 1) * P],
+                rhs=h_codes[:].bitcast(FP8X4),
+                rhs_scale=h_scale[:],
+                start=True,
+                stop=True,
+            )
+            ca = keep.tile([P, V], F32, name=f"ca{c}")
+            nc.scalar.activation(ca[:], y_bank[:], ACT.Exp, scale=0.8)
+            u = keep.tile([P, V], F32, name=f"scaled{c}")
+            nc.vector.tensor_scalar(u[:], ca[:], 0.75, inv_tot[:, c : c + 1], ALU.max, ALU.mult)
+            scaled.append(u)
+
+        for b in range(4):
+            for c in range(4):
+                nc.tensor.matmul(
+                    sums[b][:, c * P : (c + 1) * P],
+                    floor[:, c : c + 1].to_broadcast([P, P]),
+                    ident[:],
+                    is_transpose=True,
+                    start=(c == 0),
+                    stop=False,
+                )
+
+        for b in range(4):
+            backoff = keep.tile([P, S], F32, name=f"backoff{b}")
+            nc.vector.tensor_tensor(backoff[:], windows[b][:].indirect(suf_sb[:]), bow_all[:], ALU.mult)
+            for c in range(4):
+                nc.tensor.matmul(
+                    sums[b][:, c * P : (c + 1) * P],
+                    scaled[c][:, b * P : (b + 1) * P],
+                    ident[:],
+                    is_transpose=True,
+                    start=False,
+                    stop=(c == 3),
+                )
+            mixed = keep.tile([P, S], F32, name=f"mixed{b}")
+            nc.vector.tensor_tensor(mixed[:], sums[b][:], backoff[:], ALU.add)
+            logs = keep.tile([P, S], F32, name=f"logs{b}")
+            nc.scalar.activation(logs[:], mixed[:], ACT.Ln, scale=100.0, bias=0.05)
+            nc.sync.dma_start(out[b * P : (b + 1) * P, :], logs[:])

@@ -29,51 +29,53 @@ def tile_picked_ybackof_log_p_kernel(
     nc = tc.nc
     with ExitStack() as ctx:
         keep = ctx.enter_context(tc.tile_pool(name="keep", bufs=1))
-        ubanks = ctx.enter_context(tc.psum_pool(name="ubanks", bufs=4))
-        wbanks = ctx.enter_context(tc.psum_pool(name="wbanks", bufs=4))
+        banks = ctx.enter_context(tc.psum_pool(name="banks", bufs=1))
 
         low_sb = keep.tile([P, R // 16], U16, name="low_sb")
         offs_sb = keep.tile([P, S // 16], U16, name="offs_sb")
         suf_sb = keep.tile([P, S // 16], U16, name="suf_sb")
-        rows = keep.tile([P, T], F32, name="rows")
+        rows = keep.tile([P, T], F32, name="rows", tag="rows", align_bytes=64)
         e_bytes = keep.tile([P, W], U8, name="e_bytes")
         x_bytes = keep.tile([P, T], U8, name="x_bytes")
         e_table = keep.tile([P, W], I32, name="e_table")
-        x_table = keep.tile([P, T], I32, name="x_table")
+        x_table = keep.tile([P, T], I32, name="x_table", tag="x_table")
         h_raw = [keep.tile([P, PACK, HALF], F32, name=f"h_raw{h}") for h in range(2)]
         windows = [keep.tile([P, WINDOW], F32, name=f"window{b}") for b in range(4)]
         ident = keep.tile([P, P], F32, name="ident")
         warm = keep.tile([P, 1], F32, name="warm")
         warm2 = keep.tile([P, 1], F32, name="warm2")
 
-        nc.vector.memset(warm[:], 0.0)
-        nc.vector.memset(e_bytes[:].bitcast(I32), 0)
-        nc.vector.memset(x_bytes[:].bitcast(I32), 0)
+        nc.gpsimd.memset(warm[:], 0.0)
+        nc.gpsimd.memset(e_bytes[:].bitcast(I32), 0)
         nc.vector.memset(rows[:].bitcast(I32), 0)
+        nc.vector.memset(x_bytes[:].bitcast(I32), 0)
         for b in range(4):
             nc.vector.memset(windows[b][:, 2 * R : WINDOW], 0.0)
-        nc.scalar.activation(warm2[:], warm[:], ACT.Exp)
         make_identity(nc, ident[:])
 
+        def load_scales(queue, tile, scales, q):
+            queue.dma_start(tile[32 * q : 32 * q + 4, :].bitcast(I32), scales[0, 4 * q : 4 * q + 4, :].bitcast(I32))
+
         h_view = hT.rearrange("(p j) w -> p j w", j=PACK)
+        nc.scalar.activation(warm2[:], warm[:], ACT.Exp)
         nc.sync.dma_start(low_sb[:], low)
         nc.sync.dma_start(e_table[:], e_words[0].rearrange("p n t -> p (n t)").bitcast(I32))
-        for q in range(4):
-            nc.sync.dma_start(
-                e_bytes[32 * q : 32 * q + 4, :].bitcast(I32), e_scales[0, 4 * q : 4 * q + 4, :].bitcast(I32)
-            )
+        load_scales(nc.sync, e_bytes, e_scales, 0)
+        load_scales(nc.sync, e_bytes, e_scales, 1)
+        load_scales(nc.sync, e_bytes, e_scales, 2)
+        load_scales(nc.gpsimd, e_bytes, e_scales, 3)
         nc.sync.dma_start(offs_sb[:], offs)
         nc.sync.dma_start(h_raw[0][:], h_view[:, :, 0:HALF])
-        nc.scalar.dma_start(rows[TOTL_ROW : TOTL_ROW + 1, 0:W], totl[0:1, :])
-        nc.scalar.dma_start(rows[TOT_ROW : TOT_ROW + 1, :], tot[0:1, :])
-        nc.scalar.dma_start(rows[BOW_ROW : BOW_ROW + 1, :], bow[0:1, :])
+        nc.sync.dma_start(rows[TOTL_ROW : TOTL_ROW + 1, 0:W], totl[0:1, :])
+        nc.sync.dma_start(rows[TOT_ROW : TOT_ROW + 1, :], tot[0:1, :])
+        nc.sync.dma_start(rows[BOW_ROW : BOW_ROW + 1, :], bow[0:1, :])
         nc.sync.dma_start(h_raw[1][:], h_view[:, :, HALF:V])
+        load_scales(nc.sync, x_bytes, x_scales, 0)
+        load_scales(nc.sync, x_bytes, x_scales, 1)
+        load_scales(nc.sync, x_bytes, x_scales, 2)
+        load_scales(nc.sync, x_bytes, x_scales, 3)
         nc.sync.dma_start(x_table[:], x_words[0].rearrange("p n t -> p (n t)").bitcast(I32))
         nc.sync.dma_start(suf_sb[:], suf)
-        for q in range(4):
-            nc.gpsimd.dma_start(
-                x_bytes[32 * q : 32 * q + 4, :].bitcast(I32), x_scales[0, 4 * q : 4 * q + 4, :].bitcast(I32)
-            )
 
         e_codes = keep.tile([P, R], U32, name="e_codes", align_bytes=64)
         e_scale = keep.tile([P, R], U8, name="e_scale", align_bytes=64)
@@ -81,29 +83,21 @@ def tile_picked_ybackof_log_p_kernel(
         nc.vector.tensor_copy(e_scale[:], e_bytes[:].indirect(low_sb[:]))
 
         by_low = keep.tile([P, R], F32, name="by_low")
-        by_offs = keep.tile([P, S], F32, name="by_offs")
+        by_offs = keep.tile([P, S], F32, name="by_offs", tag="by_offs", align_bytes=64)
         nc.vector.tensor_copy(by_low[:], rows[:].indirect(low_sb[:]))
         nc.vector.tensor_copy(by_offs[:], rows[:].indirect(offs_sb[:]))
-        low_cols = wbanks.tile([P, 2, P], F32, name="low_cols", tag="w")
+        low_cols = banks.tile([P, 2, P], F32, name="low_cols", tag="bank0")
         for g in range(2):
             nc.tensor.transpose(low_cols[:, g, :], by_low[:, g * P : (g + 1) * P], ident[:])
-        offs_cols = wbanks.tile([P, 4, P], F32, name="offs_cols", tag="w")
+        offs_cols = banks.tile([P, 4, P], F32, name="offs_cols", tag="bank1")
         for c in range(4):
             nc.tensor.transpose(offs_cols[:, c, :], by_offs[:, c * P : (c + 1) * P], ident[:])
 
-        inv_tl = keep.tile([P, 2], F32, name="inv_tl")
-        inv_tot = keep.tile([P, 4], F32, name="inv_tot")
-        floor = keep.tile([P, 4], F32, name="floor")
-        bow_col = keep.tile([P, 4], F32, name="bow_col")
-        nc.vector.reciprocal(inv_tl[:], low_cols[:, :, TOTL_ROW])
-        nc.vector.reciprocal(inv_tot[:], offs_cols[:, :, TOT_ROW])
-        nc.scalar.copy(bow_col[:], offs_cols[:, :, BOW_ROW])
-        nc.scalar.activation(floor[:], inv_tot[:], ACT.Copy, scale=-0.75)
-
-        h_codes = keep.tile([P, V], U32, name="h_codes", align_bytes=64)
+        h_codes = keep.tile([P, V], U32, name="h_codes", tag="rows", align_bytes=64)
         h_scale = keep.tile([P, V], U8, name="h_scale", align_bytes=64)
-        for h in range(2):
-            grouped = keep.tile([P, HALF, PACK], BF16, name=f"grouped{h}", align_bytes=64)
+
+        def quantise(h):
+            grouped = keep.tile([P, HALF, PACK], BF16, name=f"grouped{h}", tag=f"grouped{h}", align_bytes=64)
             nc.scalar.copy(
                 grouped[:].rearrange("p (c i) t -> p c t i", i=4),
                 h_raw[h][:].rearrange("p t (c i) -> p c t i", i=4),
@@ -115,48 +109,76 @@ def tile_picked_ybackof_log_p_kernel(
                 in_=grouped[:].rearrange("p w j -> p (w j)"),
             )
 
-        bow_bank = wbanks.tile([P, S], F32, name="bow_bank", tag="w")
+        quantise(0)
+        inv_tl = keep.tile([P, 2], F32, name="inv_tl")
+        inv_tot = keep.tile([P, 4], F32, name="inv_tot")
+        bow_col = keep.tile([P, 4], F32, name="bow_col")
+        nc.vector.reciprocal(inv_tl[:], low_cols[:, :, TOTL_ROW])
+        nc.vector.reciprocal(inv_tot[:], offs_cols[:, :, TOT_ROW])
+        nc.scalar.copy(bow_col[:], offs_cols[:, :, BOW_ROW])
+        floor = keep.tile([P, 4], F32, name="floor")
+        nc.scalar.activation(floor[:], inv_tot[:], ACT.Copy, scale=-0.75)
+        quantise(1)
+
+        inv_tl_all = banks.tile([P, R], F32, name="inv_tl_all", tag="bank3")
+        for g in range(2):
+            nc.tensor.transpose(
+                inv_tl_all[:, g * P : (g + 1) * P], inv_tl[:, g : g + 1].to_broadcast([P, P]), ident[:]
+            )
+        bow_bank = banks.tile([P, S], F32, name="bow_bank", tag="bank2")
         for c in range(4):
             nc.tensor.transpose(bow_bank[:, c * P : (c + 1) * P], bow_col[:, c : c + 1].to_broadcast([P, P]), ident[:])
         bow_all = keep.tile([P, S], F32, name="bow_all")
         nc.scalar.copy(bow_all[:], bow_bank[:])
 
-        for h in range(2):
-            cols = slice(h * HALF, (h + 1) * HALF)
-            z_bank = wbanks.tile([P, 2, HALF], F32, name="z_bank", tag="w")
-            for g in range(2):
-                nc.tensor.matmul_mx(
-                    out=z_bank[:, g, :],
-                    lhsT=e_codes[:, g * P : (g + 1) * P].bitcast(FP8X4),
-                    lhsT_scale=e_scale[:, g * P : (g + 1) * P],
-                    rhs=h_codes[:, cols].bitcast(FP8X4),
-                    rhs_scale=h_scale[:, cols],
-                    start=True,
-                    stop=True,
-                )
-            cl = keep.tile([P, 2, HALF], F32, name=f"cl{h}")
-            nc.scalar.activation(cl[:], z_bank[:], ACT.Exp, scale=0.8)
-            plow_t = [windows[2 * h + g][:, R : 2 * R] for g in range(2)]
-            for g in range(2):
-                nc.scalar.activation(plow_t[g], cl[:, g, :], ACT.Copy, scale=inv_tl[:, g : g + 1])
-            plow_bank = wbanks.tile([P, 2, R], F32, name="plow_bank", tag="w")
-            for i in range(2):
-                for g in range(2):
-                    nc.tensor.transpose(
-                        plow_bank[:, i, g * P : (g + 1) * P], plow_t[g][:, i * P : (i + 1) * P], ident[:]
-                    )
-            for i in range(2):
-                nc.scalar.copy(windows[2 * h + i][:, 0:R], plow_bank[:, i, :])
+        z_bank = banks.tile([P, 2, R], F32, name="z_bank", tag="bank4")
+        for b in range(2):
+            nc.tensor.matmul_mx(
+                out=z_bank[:, b, :],
+                lhsT=h_codes[:, b * P : (b + 1) * P].bitcast(FP8X4),
+                lhsT_scale=h_scale[:, b * P : (b + 1) * P],
+                rhs=e_codes[:].bitcast(FP8X4),
+                rhs_scale=e_scale[:],
+                start=True,
+                stop=True,
+            )
+        for b in range(2):
+            nc.scalar.activation(windows[b][:, R : 2 * R], z_bank[:, b, :], ACT.Exp, scale=0.8)
+        for b in range(2):
+            nc.vector.tensor_tensor(windows[b][:, 0:R], windows[b][:, R : 2 * R], inv_tl_all[:], ALU.mult)
 
-        sums = [ubanks.tile([P, S], F32, name="sums", tag="u") for b in range(4)]
-        x_codes = keep.tile([P, S], U32, name="x_codes", align_bytes=64)
-        x_scale = keep.tile([P, S], U8, name="x_scale", align_bytes=64)
+        zt_bank = banks.tile([P, 2, HALF], F32, name="zt_bank", tag="bank5")
+        for g in range(2):
+            nc.tensor.matmul_mx(
+                out=zt_bank[:, g, :],
+                lhsT=e_codes[:, g * P : (g + 1) * P].bitcast(FP8X4),
+                lhsT_scale=e_scale[:, g * P : (g + 1) * P],
+                rhs=h_codes[:, HALF:V].bitcast(FP8X4),
+                rhs_scale=h_scale[:, HALF:V],
+                start=True,
+                stop=True,
+            )
+        cl_t = keep.tile([P, 2, HALF], F32, name="cl_t")
+        nc.scalar.activation(cl_t[:], zt_bank[:], ACT.Exp, scale=0.8)
+        plow_t = [windows[2 + g][:, R : 2 * R] for g in range(2)]
+        for g in range(2):
+            nc.scalar.activation(plow_t[g], cl_t[:, g, :], ACT.Copy, scale=inv_tl[:, g : g + 1])
+        plow_bank = banks.tile([P, 2, R], F32, name="plow_bank", tag="bank7")
+        for i in range(2):
+            for g in range(2):
+                nc.tensor.transpose(plow_bank[:, i, g * P : (g + 1) * P], plow_t[g][:, i * P : (i + 1) * P], ident[:])
+        for i in range(2):
+            nc.scalar.copy(windows[2 + i][:, 0:R], plow_bank[:, i, :])
+
+        x_codes = keep.tile([P, S], U32, name="x_codes", tag="grouped1", align_bytes=64)
+        x_scale = keep.tile([P, S], U8, name="x_scale", tag="by_offs", align_bytes=64)
         nc.vector.tensor_copy(x_scale[:], x_bytes[:].indirect(offs_sb[:]))
         nc.vector.tensor_copy(x_codes[:], x_table[:].bitcast(U32).indirect(offs_sb[:]))
 
+        y_tags = ["bank0", "bank1", "bank2", "bank6"]
         scaled = []
         for c in range(4):
-            y_bank = wbanks.tile([P, V], F32, name="y_bank", tag="w")
+            y_bank = banks.tile([P, V], F32, name="y_bank", tag=y_tags[c])
             nc.tensor.matmul_mx(
                 out=y_bank[:],
                 lhsT=x_codes[:, c * P : (c + 1) * P].bitcast(FP8X4),
@@ -166,12 +188,14 @@ def tile_picked_ybackof_log_p_kernel(
                 start=True,
                 stop=True,
             )
-            ca = keep.tile([P, V], F32, name=f"ca{c}")
+            ca = keep.tile([P, V], F32, name=f"ca{c}", tag=f"ca{c}")
             nc.scalar.activation(ca[:], y_bank[:], ACT.Exp, scale=0.8)
             u = keep.tile([P, V], F32, name=f"scaled{c}")
             nc.vector.tensor_scalar(u[:], ca[:], 0.75, inv_tot[:, c : c + 1], ALU.max, ALU.mult)
             scaled.append(u)
 
+        sum_tags = ["bank4", "bank5", "bank3", "bank0"]
+        sums = [banks.tile([P, S], F32, name=f"sums{b}", tag=sum_tags[b]) for b in range(4)]
         for b in range(4):
             for c in range(4):
                 nc.tensor.matmul(
@@ -182,11 +206,8 @@ def tile_picked_ybackof_log_p_kernel(
                     start=(c == 0),
                     stop=False,
                 )
-
-        for b in range(4):
-            backoff = keep.tile([P, S], F32, name=f"backoff{b}")
-            nc.vector.tensor_tensor(backoff[:], windows[b][:].indirect(suf_sb[:]), bow_all[:], ALU.mult)
-            for c in range(4):
+        for c in range(4):
+            for b in range(4):
                 nc.tensor.matmul(
                     sums[b][:, c * P : (c + 1) * P],
                     scaled[c][:, b * P : (b + 1) * P],
@@ -195,8 +216,18 @@ def tile_picked_ybackof_log_p_kernel(
                     start=False,
                     stop=(c == 3),
                 )
-            mixed = keep.tile([P, S], F32, name=f"mixed{b}")
-            nc.vector.tensor_tensor(mixed[:], sums[b][:], backoff[:], ALU.add)
-            logs = keep.tile([P, S], F32, name=f"logs{b}")
-            nc.scalar.activation(logs[:], mixed[:], ACT.Ln, scale=100.0, bias=0.05)
-            nc.sync.dma_start(out[b * P : (b + 1) * P, :], logs[:])
+
+        backoff_tags = ["backoff0", "x_table", "ca1", "ca3"]
+        backoff = [keep.tile([P, S], F32, name=f"backoff{b}", tag=backoff_tags[b]) for b in range(4)]
+        for b in range(4):
+            nc.vector.tensor_tensor(backoff[b][:], windows[b][:].indirect(suf_sb[:]), bow_all[:], ALU.mult)
+        for b in range(4):
+            pieces = 2 if b == 3 else 1
+            width = S // pieces
+            for i in range(pieces):
+                cols = slice(i * width, (i + 1) * width)
+                mixed = keep.tile([P, width], F32, name=f"mixed{b}_{i}")
+                nc.vector.tensor_tensor(mixed[:], sums[b][:, cols], backoff[b][:, cols], ALU.add)
+                logs = keep.tile([P, width], F32, name=f"logs{b}_{i}")
+                nc.scalar.activation(logs[:], mixed[:], ACT.Ln, scale=100.0, bias=0.05)
+                nc.sync.dma_start(out[b * P : (b + 1) * P, cols], logs[:])

@@ -18,9 +18,19 @@ ALU = mybir.AluOpType
 
 P = 128
 PACK = 4
+GROUP = 16
+QUADRANTS = 4
+BLOCKS = V // P
+SLABS = S // P
+LOW_SLABS = R // P
 HALF = V // 2
-WINDOW = S + 16
+WINDOW = S + GROUP
 TOT_ROW, BOW_ROW, TOTL_ROW = 0, 4, 8
+GAIN, DISCOUNT, OUT_SCALE, OUT_BIAS = 0.8, 0.75, 100.0, 0.05
+
+
+def part(i):
+    return slice(i * P, (i + 1) * P)
 
 
 def tile_picked_ybackof_log_p_kernel(
@@ -31,49 +41,55 @@ def tile_picked_ybackof_log_p_kernel(
         keep = ctx.enter_context(tc.tile_pool(name="keep", bufs=1))
         banks = ctx.enter_context(tc.psum_pool(name="banks", bufs=1))
 
-        low_sb = keep.tile([P, R // 16], U16, name="low_sb")
-        offs_sb = keep.tile([P, S // 16], U16, name="offs_sb")
-        suf_sb = keep.tile([P, S // 16], U16, name="suf_sb")
+        low_sb = keep.tile([P, R // GROUP], U16, name="low_sb")
+        offs_sb = keep.tile([P, S // GROUP], U16, name="offs_sb")
+        suf_sb = keep.tile([P, S // GROUP], U16, name="suf_sb")
         rows = keep.tile([P, T], F32, name="rows", tag="rows", align_bytes=64)
         e_bytes = keep.tile([P, W], U8, name="e_bytes")
         x_bytes = keep.tile([P, T], U8, name="x_bytes")
         e_table = keep.tile([P, W], I32, name="e_table")
         x_table = keep.tile([P, T], I32, name="x_table", tag="x_table")
         h_raw = [keep.tile([P, PACK, HALF], F32, name=f"h_raw{h}") for h in range(2)]
-        windows = [keep.tile([P, WINDOW], F32, name=f"window{b}") for b in range(4)]
+        windows = [keep.tile([P, WINDOW], F32, name=f"window{b}") for b in range(BLOCKS)]
         ident = keep.tile([P, P], F32, name="ident")
-        warm = keep.tile([P, 1], F32, name="warm")
-        warm2 = keep.tile([P, 1], F32, name="warm2")
 
-        nc.gpsimd.memset(warm[:], 0.0)
         nc.gpsimd.memset(e_bytes[:].bitcast(I32), 0)
         nc.vector.memset(rows[:].bitcast(I32), 0)
         nc.vector.memset(x_bytes[:].bitcast(I32), 0)
-        for b in range(4):
+        for b in range(BLOCKS):
             nc.vector.memset(windows[b][:, 2 * R : WINDOW], 0.0)
         make_identity(nc, ident[:])
 
         def load_scales(queue, tile, scales, q):
             queue.dma_start(tile[32 * q : 32 * q + 4, :].bitcast(I32), scales[0, 4 * q : 4 * q + 4, :].bitcast(I32))
 
+        def spread(column):
+            return column.to_broadcast([P, P])
+
+        def product(result, stationary, moving):
+            nc.tensor.matmul_mx(
+                out=result,
+                lhsT=stationary[0].bitcast(FP8X4),
+                lhsT_scale=stationary[1],
+                rhs=moving[0].bitcast(FP8X4),
+                rhs_scale=moving[1],
+                start=True,
+                stop=True,
+            )
+
         h_view = hT.rearrange("(p j) w -> p j w", j=PACK)
-        nc.scalar.activation(warm2[:], warm[:], ACT.Exp)
         nc.sync.dma_start(low_sb[:], low)
         nc.sync.dma_start(e_table[:], e_words[0].rearrange("p n t -> p (n t)").bitcast(I32))
-        load_scales(nc.sync, e_bytes, e_scales, 0)
-        load_scales(nc.sync, e_bytes, e_scales, 1)
-        load_scales(nc.sync, e_bytes, e_scales, 2)
-        load_scales(nc.gpsimd, e_bytes, e_scales, 3)
+        for q in range(QUADRANTS):
+            load_scales(nc.gpsimd if q == QUADRANTS - 1 else nc.sync, e_bytes, e_scales, q)
         nc.sync.dma_start(offs_sb[:], offs)
         nc.sync.dma_start(h_raw[0][:], h_view[:, :, 0:HALF])
         nc.sync.dma_start(rows[TOTL_ROW : TOTL_ROW + 1, 0:W], totl[0:1, :])
         nc.sync.dma_start(rows[TOT_ROW : TOT_ROW + 1, :], tot[0:1, :])
         nc.sync.dma_start(rows[BOW_ROW : BOW_ROW + 1, :], bow[0:1, :])
         nc.sync.dma_start(h_raw[1][:], h_view[:, :, HALF:V])
-        load_scales(nc.sync, x_bytes, x_scales, 0)
-        load_scales(nc.sync, x_bytes, x_scales, 1)
-        load_scales(nc.sync, x_bytes, x_scales, 2)
-        load_scales(nc.sync, x_bytes, x_scales, 3)
+        for q in range(QUADRANTS):
+            load_scales(nc.sync, x_bytes, x_scales, q)
         nc.sync.dma_start(x_table[:], x_words[0].rearrange("p n t -> p (n t)").bitcast(I32))
         nc.sync.dma_start(suf_sb[:], suf)
 
@@ -86,12 +102,12 @@ def tile_picked_ybackof_log_p_kernel(
         by_offs = keep.tile([P, S], F32, name="by_offs", tag="by_offs", align_bytes=64)
         nc.vector.tensor_copy(by_low[:], rows[:].indirect(low_sb[:]))
         nc.vector.tensor_copy(by_offs[:], rows[:].indirect(offs_sb[:]))
-        low_cols = banks.tile([P, 2, P], F32, name="low_cols", tag="bank0")
-        for g in range(2):
-            nc.tensor.transpose(low_cols[:, g, :], by_low[:, g * P : (g + 1) * P], ident[:])
-        offs_cols = banks.tile([P, 4, P], F32, name="offs_cols", tag="bank1")
-        for c in range(4):
-            nc.tensor.transpose(offs_cols[:, c, :], by_offs[:, c * P : (c + 1) * P], ident[:])
+        low_cols = banks.tile([P, LOW_SLABS, P], F32, name="low_cols", tag="bank0")
+        for g in range(LOW_SLABS):
+            nc.tensor.transpose(low_cols[:, g, :], by_low[:, part(g)], ident[:])
+        offs_cols = banks.tile([P, SLABS, P], F32, name="offs_cols", tag="bank1")
+        for c in range(SLABS):
+            nc.tensor.transpose(offs_cols[:, c, :], by_offs[:, part(c)], ident[:])
 
         h_codes = keep.tile([P, V], U32, name="h_codes", tag="rows", align_bytes=64)
         h_scale = keep.tile([P, V], U8, name="h_scale", align_bytes=64)
@@ -110,63 +126,47 @@ def tile_picked_ybackof_log_p_kernel(
             )
 
         quantise(0)
-        inv_tl = keep.tile([P, 2], F32, name="inv_tl")
-        inv_tot = keep.tile([P, 4], F32, name="inv_tot")
-        bow_col = keep.tile([P, 4], F32, name="bow_col")
+        inv_tl = keep.tile([P, LOW_SLABS], F32, name="inv_tl")
+        inv_tot = keep.tile([P, SLABS], F32, name="inv_tot")
+        bow_col = keep.tile([P, SLABS], F32, name="bow_col")
         nc.vector.reciprocal(inv_tl[:], low_cols[:, :, TOTL_ROW])
         nc.vector.reciprocal(inv_tot[:], offs_cols[:, :, TOT_ROW])
         nc.scalar.copy(bow_col[:], offs_cols[:, :, BOW_ROW])
-        floor = keep.tile([P, 4], F32, name="floor")
-        nc.scalar.activation(floor[:], inv_tot[:], ACT.Copy, scale=-0.75)
+        floor = keep.tile([P, SLABS], F32, name="floor")
+        nc.scalar.activation(floor[:], inv_tot[:], ACT.Copy, scale=-DISCOUNT)
         quantise(1)
 
         inv_tl_all = banks.tile([P, R], F32, name="inv_tl_all", tag="bank3")
-        for g in range(2):
-            nc.tensor.transpose(
-                inv_tl_all[:, g * P : (g + 1) * P], inv_tl[:, g : g + 1].to_broadcast([P, P]), ident[:]
-            )
+        for g in range(LOW_SLABS):
+            nc.tensor.transpose(inv_tl_all[:, part(g)], spread(inv_tl[:, g : g + 1]), ident[:])
         bow_bank = banks.tile([P, S], F32, name="bow_bank", tag="bank2")
-        for c in range(4):
-            nc.tensor.transpose(bow_bank[:, c * P : (c + 1) * P], bow_col[:, c : c + 1].to_broadcast([P, P]), ident[:])
+        for c in range(SLABS):
+            nc.tensor.transpose(bow_bank[:, part(c)], spread(bow_col[:, c : c + 1]), ident[:])
         bow_all = keep.tile([P, S], F32, name="bow_all")
         nc.scalar.copy(bow_all[:], bow_bank[:])
 
         z_bank = banks.tile([P, 2, R], F32, name="z_bank", tag="bank4")
         for b in range(2):
-            nc.tensor.matmul_mx(
-                out=z_bank[:, b, :],
-                lhsT=h_codes[:, b * P : (b + 1) * P].bitcast(FP8X4),
-                lhsT_scale=h_scale[:, b * P : (b + 1) * P],
-                rhs=e_codes[:].bitcast(FP8X4),
-                rhs_scale=e_scale[:],
-                start=True,
-                stop=True,
-            )
+            product(z_bank[:, b, :], (h_codes[:, part(b)], h_scale[:, part(b)]), (e_codes[:], e_scale[:]))
         for b in range(2):
-            nc.scalar.activation(windows[b][:, R : 2 * R], z_bank[:, b, :], ACT.Exp, scale=0.8)
+            nc.scalar.activation(windows[b][:, R : 2 * R], z_bank[:, b, :], ACT.Exp, scale=GAIN)
         for b in range(2):
             nc.vector.tensor_tensor(windows[b][:, 0:R], windows[b][:, R : 2 * R], inv_tl_all[:], ALU.mult)
 
-        zt_bank = banks.tile([P, 2, HALF], F32, name="zt_bank", tag="bank5")
-        for g in range(2):
-            nc.tensor.matmul_mx(
-                out=zt_bank[:, g, :],
-                lhsT=e_codes[:, g * P : (g + 1) * P].bitcast(FP8X4),
-                lhsT_scale=e_scale[:, g * P : (g + 1) * P],
-                rhs=h_codes[:, HALF:V].bitcast(FP8X4),
-                rhs_scale=h_scale[:, HALF:V],
-                start=True,
-                stop=True,
+        zt_bank = banks.tile([P, LOW_SLABS, HALF], F32, name="zt_bank", tag="bank5")
+        for g in range(LOW_SLABS):
+            product(
+                zt_bank[:, g, :], (e_codes[:, part(g)], e_scale[:, part(g)]), (h_codes[:, HALF:V], h_scale[:, HALF:V])
             )
-        cl_t = keep.tile([P, 2, HALF], F32, name="cl_t")
-        nc.scalar.activation(cl_t[:], zt_bank[:], ACT.Exp, scale=0.8)
-        plow_t = [windows[2 + g][:, R : 2 * R] for g in range(2)]
-        for g in range(2):
+        cl_t = keep.tile([P, LOW_SLABS, HALF], F32, name="cl_t")
+        nc.scalar.activation(cl_t[:], zt_bank[:], ACT.Exp, scale=GAIN)
+        plow_t = [windows[2 + g][:, R : 2 * R] for g in range(LOW_SLABS)]
+        for g in range(LOW_SLABS):
             nc.scalar.activation(plow_t[g], cl_t[:, g, :], ACT.Copy, scale=inv_tl[:, g : g + 1])
         plow_bank = banks.tile([P, 2, R], F32, name="plow_bank", tag="bank7")
         for i in range(2):
-            for g in range(2):
-                nc.tensor.transpose(plow_bank[:, i, g * P : (g + 1) * P], plow_t[g][:, i * P : (i + 1) * P], ident[:])
+            for g in range(LOW_SLABS):
+                nc.tensor.transpose(plow_bank[:, i, part(g)], plow_t[g][:, part(i)], ident[:])
         for i in range(2):
             nc.scalar.copy(windows[2 + i][:, 0:R], plow_bank[:, i, :])
 
@@ -177,57 +177,49 @@ def tile_picked_ybackof_log_p_kernel(
 
         y_tags = ["bank0", "bank1", "bank2", "bank6"]
         scaled = []
-        for c in range(4):
+        for c in range(SLABS):
             y_bank = banks.tile([P, V], F32, name="y_bank", tag=y_tags[c])
-            nc.tensor.matmul_mx(
-                out=y_bank[:],
-                lhsT=x_codes[:, c * P : (c + 1) * P].bitcast(FP8X4),
-                lhsT_scale=x_scale[:, c * P : (c + 1) * P],
-                rhs=h_codes[:].bitcast(FP8X4),
-                rhs_scale=h_scale[:],
-                start=True,
-                stop=True,
-            )
+            product(y_bank[:], (x_codes[:, part(c)], x_scale[:, part(c)]), (h_codes[:], h_scale[:]))
             ca = keep.tile([P, V], F32, name=f"ca{c}", tag=f"ca{c}")
-            nc.scalar.activation(ca[:], y_bank[:], ACT.Exp, scale=0.8)
-            u = keep.tile([P, V], F32, name=f"scaled{c}")
-            nc.vector.tensor_scalar(u[:], ca[:], 0.75, inv_tot[:, c : c + 1], ALU.max, ALU.mult)
-            scaled.append(u)
+            nc.scalar.activation(ca[:], y_bank[:], ACT.Exp, scale=GAIN)
+            scaled.append(keep.tile([P, V], F32, name=f"scaled{c}"))
+            nc.vector.tensor_scalar(scaled[c][:], ca[:], DISCOUNT, inv_tot[:, c : c + 1], ALU.max, ALU.mult)
 
-        sum_tags = ["bank4", "bank5", "bank3", "bank0"]
-        sums = [banks.tile([P, S], F32, name=f"sums{b}", tag=sum_tags[b]) for b in range(4)]
-        for b in range(4):
-            for c in range(4):
+        share_tags = ["bank4", "bank5", "bank3", "bank0"]
+        share = [banks.tile([P, S], F32, name=f"share{b}", tag=share_tags[b]) for b in range(BLOCKS)]
+        for b in range(BLOCKS):
+            for c in range(SLABS):
                 nc.tensor.matmul(
-                    sums[b][:, c * P : (c + 1) * P],
-                    floor[:, c : c + 1].to_broadcast([P, P]),
+                    share[b][:, part(c)],
+                    spread(floor[:, c : c + 1]),
                     ident[:],
                     is_transpose=True,
                     start=(c == 0),
                     stop=False,
                 )
-        for c in range(4):
-            for b in range(4):
+        for c in range(SLABS):
+            for b in range(BLOCKS):
                 nc.tensor.matmul(
-                    sums[b][:, c * P : (c + 1) * P],
-                    scaled[c][:, b * P : (b + 1) * P],
+                    share[b][:, part(c)],
+                    scaled[c][:, part(b)],
                     ident[:],
                     is_transpose=True,
                     start=False,
-                    stop=(c == 3),
+                    stop=(c == SLABS - 1),
                 )
 
         backoff_tags = ["backoff0", "x_table", "ca1", "ca3"]
-        backoff = [keep.tile([P, S], F32, name=f"backoff{b}", tag=backoff_tags[b]) for b in range(4)]
-        for b in range(4):
+        backoff = [keep.tile([P, S], F32, name=f"backoff{b}", tag=backoff_tags[b]) for b in range(BLOCKS)]
+        for b in range(BLOCKS):
             nc.vector.tensor_tensor(backoff[b][:], windows[b][:].indirect(suf_sb[:]), bow_all[:], ALU.mult)
-        for b in range(4):
-            pieces = 2 if b == 3 else 1
+
+        for b in range(BLOCKS):
+            pieces = 2 if b == BLOCKS - 1 else 1
             width = S // pieces
             for i in range(pieces):
                 cols = slice(i * width, (i + 1) * width)
                 mixed = keep.tile([P, width], F32, name=f"mixed{b}_{i}")
-                nc.vector.tensor_tensor(mixed[:], sums[b][:, cols], backoff[b][:, cols], ALU.add)
+                nc.vector.tensor_tensor(mixed[:], share[b][:, cols], backoff[b][:, cols], ALU.add)
                 logs = keep.tile([P, width], F32, name=f"logs{b}_{i}")
-                nc.scalar.activation(logs[:], mixed[:], ACT.Ln, scale=100.0, bias=0.05)
-                nc.sync.dma_start(out[b * P : (b + 1) * P, cols], logs[:])
+                nc.scalar.activation(logs[:], mixed[:], ACT.Ln, scale=OUT_SCALE, bias=OUT_BIAS)
+                nc.sync.dma_start(out[part(b), cols], logs[:])

from contextlib import ExitStack

import concourse.mybir as mybir
from concourse.masks import make_identity

K, T, S, V, R, W = 512, 2048, 512, 512, 256, 1024
FLOPS = 2 * K * V * (S + R)

F32 = mybir.dt.float32
BF16 = mybir.dt.bfloat16
I32 = mybir.dt.int32
U32 = mybir.dt.uint32
U16 = mybir.dt.uint16
U8 = mybir.dt.uint8
FP8X4 = mybir.dt.float8_e4m3fn_x4
ACT = mybir.ActivationFunctionType
ALU = mybir.AluOpType

P = 128
PACK = 4
GROUP = 16
QUADRANTS = 4
BLOCKS = V // P
SLABS = S // P
LOW_SLABS = R // P
HALF = V // 2
WINDOW = S + GROUP
TOT_ROW, BOW_ROW, TOTL_ROW = 0, 4, 8
GAIN, DISCOUNT, OUT_SCALE, OUT_BIAS = 0.8, 0.75, 100.0, 0.05


def part(i):
    return slice(i * P, (i + 1) * P)


def tile_picked_ybackof_log_p_kernel(
    tc, x_words, x_scales, hT, e_words, e_scales, totl, bow, tot, offs, low, suf, out
):
    nc = tc.nc
    with ExitStack() as ctx:
        keep = ctx.enter_context(tc.tile_pool(name="keep", bufs=1))
        banks = ctx.enter_context(tc.psum_pool(name="banks", bufs=1))

        low_sb = keep.tile([P, R // GROUP], U16, name="low_sb")
        offs_sb = keep.tile([P, S // GROUP], U16, name="offs_sb")
        suf_sb = keep.tile([P, S // GROUP], U16, name="suf_sb")
        rows = keep.tile([P, T], F32, name="rows", tag="rows", align_bytes=64)
        e_bytes = keep.tile([P, W], U8, name="e_bytes")
        x_bytes = keep.tile([P, T], U8, name="x_bytes")
        e_table = keep.tile([P, W], I32, name="e_table")
        x_table = keep.tile([P, T], I32, name="x_table", tag="x_table")
        h_raw = [keep.tile([P, PACK, HALF], F32, name=f"h_raw{h}") for h in range(2)]
        windows = [keep.tile([P, WINDOW], F32, name=f"window{b}") for b in range(BLOCKS)]
        ident = keep.tile([P, P], F32, name="ident")

        nc.gpsimd.memset(e_bytes[:].bitcast(I32), 0)
        nc.vector.memset(rows[:].bitcast(I32), 0)
        nc.vector.memset(x_bytes[:].bitcast(I32), 0)
        for b in range(BLOCKS):
            nc.vector.memset(windows[b][:, 2 * R : WINDOW], 0.0)
        make_identity(nc, ident[:])

        def load_scales(queue, tile, scales, q):
            queue.dma_start(tile[32 * q : 32 * q + 4, :].bitcast(I32), scales[0, 4 * q : 4 * q + 4, :].bitcast(I32))

        def spread(column):
            return column.to_broadcast([P, P])

        def product(result, stationary, moving):
            nc.tensor.matmul_mx(
                out=result,
                lhsT=stationary[0].bitcast(FP8X4),
                lhsT_scale=stationary[1],
                rhs=moving[0].bitcast(FP8X4),
                rhs_scale=moving[1],
                start=True,
                stop=True,
            )

        h_view = hT.rearrange("(p j) w -> p j w", j=PACK)
        nc.sync.dma_start(low_sb[:], low)
        nc.sync.dma_start(e_table[:], e_words[0].rearrange("p n t -> p (n t)").bitcast(I32))
        for q in range(QUADRANTS):
            load_scales(nc.gpsimd if q == QUADRANTS - 1 else nc.sync, e_bytes, e_scales, q)
        nc.sync.dma_start(offs_sb[:], offs)
        nc.sync.dma_start(h_raw[0][:], h_view[:, :, 0:HALF])
        nc.sync.dma_start(rows[TOTL_ROW : TOTL_ROW + 1, 0:W], totl[0:1, :])
        nc.sync.dma_start(rows[TOT_ROW : TOT_ROW + 1, :], tot[0:1, :])
        nc.sync.dma_start(rows[BOW_ROW : BOW_ROW + 1, :], bow[0:1, :])
        nc.sync.dma_start(h_raw[1][:], h_view[:, :, HALF:V])
        for q in range(QUADRANTS):
            load_scales(nc.sync, x_bytes, x_scales, q)
        nc.sync.dma_start(x_table[:], x_words[0].rearrange("p n t -> p (n t)").bitcast(I32))
        nc.sync.dma_start(suf_sb[:], suf)

        e_codes = keep.tile([P, R], U32, name="e_codes", align_bytes=64)
        e_scale = keep.tile([P, R], U8, name="e_scale", align_bytes=64)
        nc.vector.tensor_copy(e_codes[:], e_table[:].bitcast(U32).indirect(low_sb[:]))
        nc.vector.tensor_copy(e_scale[:], e_bytes[:].indirect(low_sb[:]))

        by_low = keep.tile([P, R], F32, name="by_low")
        by_offs = keep.tile([P, S], F32, name="by_offs", tag="by_offs", align_bytes=64)
        nc.vector.tensor_copy(by_low[:], rows[:].indirect(low_sb[:]))
        nc.vector.tensor_copy(by_offs[:], rows[:].indirect(offs_sb[:]))
        low_cols = banks.tile([P, LOW_SLABS, P], F32, name="low_cols", tag="bank0")
        for g in range(LOW_SLABS):
            nc.tensor.transpose(low_cols[:, g, :], by_low[:, part(g)], ident[:])
        offs_cols = banks.tile([P, SLABS, P], F32, name="offs_cols", tag="bank1")
        for c in range(SLABS):
            nc.tensor.transpose(offs_cols[:, c, :], by_offs[:, part(c)], ident[:])

        h_codes = keep.tile([P, V], U32, name="h_codes", tag="rows", align_bytes=64)
        h_scale = keep.tile([P, V], U8, name="h_scale", align_bytes=64)

        def quantise(h):
            grouped = keep.tile([P, HALF, PACK], BF16, name=f"grouped{h}", tag=f"grouped{h}", align_bytes=64)
            nc.scalar.copy(
                grouped[:].rearrange("p (c i) t -> p c t i", i=4),
                h_raw[h][:].rearrange("p t (c i) -> p c t i", i=4),
            )
            cols = slice(h * HALF, (h + 1) * HALF)
            nc.vector.quantize_mx(
                out=h_codes[:, cols].bitcast(FP8X4),
                scales=h_scale[:, cols],
                in_=grouped[:].rearrange("p w j -> p (w j)"),
            )

        quantise(0)
        inv_tl = keep.tile([P, LOW_SLABS], F32, name="inv_tl")
        inv_tot = keep.tile([P, SLABS], F32, name="inv_tot")
        bow_col = keep.tile([P, SLABS], F32, name="bow_col")
        nc.vector.reciprocal(inv_tl[:], low_cols[:, :, TOTL_ROW])
        nc.vector.reciprocal(inv_tot[:], offs_cols[:, :, TOT_ROW])
        nc.scalar.copy(bow_col[:], offs_cols[:, :, BOW_ROW])
        floor = keep.tile([P, SLABS], F32, name="floor")
        nc.scalar.activation(floor[:], inv_tot[:], ACT.Copy, scale=-DISCOUNT)
        quantise(1)

        inv_tl_all = banks.tile([P, R], F32, name="inv_tl_all", tag="bank3")
        for g in range(LOW_SLABS):
            nc.tensor.transpose(inv_tl_all[:, part(g)], spread(inv_tl[:, g : g + 1]), ident[:])
        bow_bank = banks.tile([P, S], F32, name="bow_bank", tag="bank2")
        for c in range(SLABS):
            nc.tensor.transpose(bow_bank[:, part(c)], spread(bow_col[:, c : c + 1]), ident[:])
        bow_all = keep.tile([P, S], F32, name="bow_all")
        nc.scalar.copy(bow_all[:], bow_bank[:])

        z_bank = banks.tile([P, 2, R], F32, name="z_bank", tag="bank4")
        for b in range(2):
            product(z_bank[:, b, :], (h_codes[:, part(b)], h_scale[:, part(b)]), (e_codes[:], e_scale[:]))
        for b in range(2):
            nc.scalar.activation(windows[b][:, R : 2 * R], z_bank[:, b, :], ACT.Exp, scale=GAIN)
        for b in range(2):
            nc.vector.tensor_tensor(windows[b][:, 0:R], windows[b][:, R : 2 * R], inv_tl_all[:], ALU.mult)

        zt_bank = banks.tile([P, LOW_SLABS, HALF], F32, name="zt_bank", tag="bank5")
        for g in range(LOW_SLABS):
            product(
                zt_bank[:, g, :], (e_codes[:, part(g)], e_scale[:, part(g)]), (h_codes[:, HALF:V], h_scale[:, HALF:V])
            )
        cl_t = keep.tile([P, LOW_SLABS, HALF], F32, name="cl_t")
        nc.scalar.activation(cl_t[:], zt_bank[:], ACT.Exp, scale=GAIN)
        plow_t = [windows[2 + g][:, R : 2 * R] for g in range(LOW_SLABS)]
        for g in range(LOW_SLABS):
            nc.scalar.activation(plow_t[g], cl_t[:, g, :], ACT.Copy, scale=inv_tl[:, g : g + 1])
        plow_bank = banks.tile([P, 2, R], F32, name="plow_bank", tag="bank7")
        for i in range(2):
            for g in range(LOW_SLABS):
                nc.tensor.transpose(plow_bank[:, i, part(g)], plow_t[g][:, part(i)], ident[:])
        for i in range(2):
            nc.scalar.copy(windows[2 + i][:, 0:R], plow_bank[:, i, :])

        x_codes = keep.tile([P, S], U32, name="x_codes", tag="grouped1", align_bytes=64)
        x_scale = keep.tile([P, S], U8, name="x_scale", tag="by_offs", align_bytes=64)
        nc.vector.tensor_copy(x_scale[:], x_bytes[:].indirect(offs_sb[:]))
        nc.vector.tensor_copy(x_codes[:], x_table[:].bitcast(U32).indirect(offs_sb[:]))

        y_tags = ["bank0", "bank1", "bank2", "bank6"]
        scaled = []
        for c in range(SLABS):
            y_bank = banks.tile([P, V], F32, name="y_bank", tag=y_tags[c])
            product(y_bank[:], (x_codes[:, part(c)], x_scale[:, part(c)]), (h_codes[:], h_scale[:]))
            ca = keep.tile([P, V], F32, name=f"ca{c}", tag=f"ca{c}")
            nc.scalar.activation(ca[:], y_bank[:], ACT.Exp, scale=GAIN)
            scaled.append(keep.tile([P, V], F32, name=f"scaled{c}"))
            nc.vector.tensor_scalar(scaled[c][:], ca[:], DISCOUNT, inv_tot[:, c : c + 1], ALU.max, ALU.mult)

        share_tags = ["bank4", "bank5", "bank3", "bank0"]
        share = [banks.tile([P, S], F32, name=f"share{b}", tag=share_tags[b]) for b in range(BLOCKS)]
        for b in range(BLOCKS):
            for c in range(SLABS):
                nc.tensor.matmul(
                    share[b][:, part(c)],
                    spread(floor[:, c : c + 1]),
                    ident[:],
                    is_transpose=True,
                    start=(c == 0),
                    stop=False,
                )
        for c in range(SLABS):
            for b in range(BLOCKS):
                nc.tensor.matmul(
                    share[b][:, part(c)],
                    scaled[c][:, part(b)],
                    ident[:],
                    is_transpose=True,
                    start=False,
                    stop=(c == SLABS - 1),
                )

        backoff_tags = ["backoff0", "x_table", "ca1", "ca3"]
        backoff = [keep.tile([P, S], F32, name=f"backoff{b}", tag=backoff_tags[b]) for b in range(BLOCKS)]
        for b in range(BLOCKS):
            nc.vector.tensor_tensor(backoff[b][:], windows[b][:].indirect(suf_sb[:]), bow_all[:], ALU.mult)

        for b in range(BLOCKS):
            pieces = 2 if b == BLOCKS - 1 else 1
            width = S // pieces
            for i in range(pieces):
                cols = slice(i * width, (i + 1) * width)
                mixed = keep.tile([P, width], F32, name=f"mixed{b}_{i}")
                nc.vector.tensor_tensor(mixed[:], share[b][:, cols], backoff[b][:, cols], ALU.add)
                logs = keep.tile([P, width], F32, name=f"logs{b}_{i}")
                nc.scalar.activation(logs[:], mixed[:], ACT.Ln, scale=OUT_SCALE, bias=OUT_BIAS)
                nc.sync.dma_start(out[part(b), cols], logs[:])
